import numpy as np, ml_dtypes
CORES = [2,3,42,43,82,83,122,123]
N = 8
K, F = 3, 128
def setup_inputs(rng):
    return {"gr": rng.standard_normal((N, K, 128, N * F), dtype=np.float32).astype(ml_dtypes.bfloat16)}
def setup_inputs_big(rng):
    d = setup_inputs(rng)
    for k in ("gr",): d[k] = (d[k].astype(np.float32) * 1048576.0).astype(d[k].dtype)
    return d
def setup_inputs_small(rng):
    d = setup_inputs(rng)
    for k in ("gr",): d[k] = (d[k].astype(np.float32) * (1 / 1048576.0)).astype(d[k].dtype)
    return d
def reference(gr):
    s = gr.astype(np.float64).sum(axis=(0, 1))
    return {"y": np.stack([s[:, F * r:F * r + F] for r in range(N)]).astype(np.float32 if gr.dtype != np.float64 else np.float64)}

@@ -1,0 +1,171 @@
+from concourse.mybir import AluOpType
+
+F = 128
+KT = 3
+NB = 8
+W = NB * F
+
+SCRATCH = {
+    "tab": ("sbuf", [128, KT * W], "bfloat16"),
+    "u": ("sbuf", [128, W], "float32"),
+    "st": ("sbuf", [128, 3 * F], "float32"),
+    "st2": ("sbuf", [128, F], "float32"),
+    "m": ("sbuf", [128, 4 * F], "float32"),
+    "m2": ("sbuf", [128, F], "float32"),
+    "rawl": ("sbuf", [128, F], "bfloat16"),
+    "xl": ("sbuf", [128, 3 * F], "float32"),
+    "xl2": ("sbuf", [128, F], "float32"),
+    "out": ("sbuf", [128, 3 * F], "float32"),
+    "al": ("sbuf", [128, 3 * F], "float32"),
+    "acc": ("sbuf", [128, 4 * F], "float32"),
+}
+SEMAPHORES = ["lc0", "lc1", "lc2", "lr0", "lr1", "lr2", "vq", "sst", "sst2", "xraw", "x1", "x2",
+              "os0", "os1", "os2", "ar0", "ar1", "ar2", "sacc", "stored", "sent"]
+
+
+def _runs(blocks):
+    res = []
+    for pos, b in enumerate(blocks):
+        if res and res[-1][0] + res[-1][1] == b:
+            res[-1][1] += 1
+        else:
+            res.append([b, 1, pos])
+    return res
+
+
+def _plan(T, topo):
+    cores = list(T.cores)
+    n = len(cores)
+    bychip = {}
+    for r, c in enumerate(cores):
+        bychip.setdefault(topo.chip(c), []).append(r)
+    info = {}
+    for ch, (ra, rb) in bychip.items():
+        off = [r for r in range(n) if r not in (ra, rb)]
+        lo, hi = off[:len(off) // 2], off[len(off) // 2:]
+        if hi[0] > rb:
+            three, five, p3, p5 = hi, lo, (hi[0], n), (0, hi[0])
+        else:
+            three, five, p3, p5 = lo, hi, (0, lo[-1] + 1), (lo[-1] + 1, n)
+        info[ra] = dict(peer=rb, mine=three, theirs=five, crit=p5, rest=p3)
+        info[rb] = dict(peer=ra, mine=five, theirs=three, crit=p3, rest=p5)
+    arrivals = {d: [] for d in range(n)}
+    for r in range(n):
+        me = topo.chip(cores[r])
+        mine = info[r]["mine"]
+        order = sorted(range(len(mine)), key=lambda j: (topo.same_plane(me, topo.chip(cores[mine[j]])), mine[j]))
+        info[r]["order"] = order
+        for pos, j in enumerate(order):
+            arrivals[mine[j]].append((pos, r))
+    slot = {}
+    for d in range(n):
+        for s, (pos, r) in enumerate(sorted(arrivals[d])):
+            slot[(r, d)] = s
+    return info, slot
+
+
+def rank_program(g, core, T, topo):
+    rank = T.rank_of(core)
+    if rank is None:
+        return
+    cores = list(T.cores)
+    info, slot = _plan(T, topo)
+    me = info[rank]
+    peer, mine, theirs, order = me["peer"], me["mine"], me["theirs"], me["order"]
+    pcore = cores[peer]
+    S = T.sem
+    add = AluOpType.add
+    v = g.vector
+
+    def tab(k, b, nb=1):
+        return T.tab[:, k * W + b * F: k * W + (b + nb) * F]
+
+    def blk(buf, pos, nb=1):
+        return buf[:, pos * F:(pos + nb) * F]
+
+    (c0, c1), (r0, r1) = me["crit"], me["rest"]
+    jobs = [(g.sync, 0, c0, c1, S.lc0), (g.scalar, 1, c0, c1, S.lc1), (g.sync, 2, c0, c1, S.lc2),
+            (g.scalar, 0, r0, r1, S.lr0), (g.sync, 1, r0, r1, S.lr1), (g.scalar, 2, r0, r1, S.lr2)]
+    for q, k, b0, b1, sem in jobs:
+        q.dma_start(out=tab(k, b0, b1 - b0), in_=T.gr[k, :, b0 * F:b1 * F]).then_inc(sem, 16)
+
+    off_mask = topo.mask(core, cores[mine[0]])
+    for d in mine:
+        off_mask &= topo.mask(core, cores[d])
+    on_mask = topo.mask(core, pcore) & off_mask
+    n_on = bin(on_mask).count("1")
+    n_off = bin(off_mask).count("1")
+    sent = [0]
+
+    def send(dst_core, out_ap, in_ap, sem, mask):
+        assert topo.may_write(core, dst_core)
+        rid, pid, _se = topo.addr(dst_core)
+        g.remote_dma(out_ap=out_ap, in_ap=in_ap, remote_sem=sem, local_sem=S.sent, pid=pid, routing_id=rid,
+                     dma_engine_mask=mask)
+        sent[0] += bin(mask).count("1")
+
+    g.wait_ge(S.lc0, 16)
+    send(pcore, T.rawl[:, :], tab(0, theirs[0]), S.xraw, on_mask)
+
+    nv = [0]
+    late = _runs(theirs[1:])
+    v.wait_ge(S.lc0, 16)
+    v.wait_ge(S.lc1, 16)
+    for b, nb, pos in late:
+        v.tensor_tensor(out=blk(T.u, b, nb), in0=tab(0, b, nb), in1=tab(1, b, nb), op=add).then_inc(S.vq, 1)
+        nv[0] += 1
+    v.wait_ge(S.lc2, 16)
+    v.tensor_tensor(out=blk(T.st, 0), in0=tab(1, theirs[0]), in1=tab(2, theirs[0]), op=add).then_inc(S.sst, 1)
+    v.wait_ge(S.vq, nv[0])
+    for b, nb, pos in late:
+        v.tensor_tensor(out=blk(T.st, pos + 1, nb), in0=blk(T.u, b, nb), in1=tab(2, b, nb), op=add).then_inc(S.sst, 1)
+    g.wait_ge(S.sst, 1 + len(late))
+    send(pcore, T.xl[:, :], T.st[:, :], S.x1, on_mask)
+
+    rem = _runs(sorted(mine + [rank, peer]))
+    v.wait_ge(S.lr0, 16)
+    v.wait_ge(S.lr1, 16)
+    for b, nb, pos in rem:
+        v.tensor_tensor(out=blk(T.u, b, nb), in0=tab(0, b, nb), in1=tab(1, b, nb), op=add).then_inc(S.vq, 1)
+        nv[0] += 1
+    v.wait_ge(S.lr2, 16)
+    v.wait_ge(S.vq, nv[0])
+    v.tensor_tensor(out=T.st2[:, :], in0=blk(T.u, peer), in1=tab(2, peer), op=add).then_inc(S.sst2, 1)
+    g.wait_ge(S.sst2, 1)
+    send(pcore, T.xl2[:, :], T.st2[:, :], S.x2, on_mask)
+    for b, nb, pos in _runs(mine):
+        v.tensor_tensor(out=blk(T.m, pos, nb), in0=blk(T.u, b, nb), in1=tab(2, b, nb), op=add).then_inc(S.vq, 1)
+        nv[0] += 1
+    v.tensor_tensor(out=blk(T.m, 3), in0=blk(T.u, rank), in1=tab(2, rank), op=add).then_inc(S.vq, 1)
+    nv[0] += 1
+
+    v.wait_ge(S.xraw, n_on)
+    v.wait_ge(S.vq, nv[0])
+    v.tensor_tensor(out=T.m2[:, :], in0=blk(T.m, 0), in1=T.rawl[:, :], op=add).then_inc(S.vq, 1)
+    nv[0] += 1
+    v.wait_ge(S.x1, n_on)
+    v.wait_ge(S.vq, nv[0])
+    for j in order:
+        src = T.m2[:, :] if j == 0 else blk(T.m, j)
+        v.tensor_tensor(out=blk(T.out, j), in0=src, in1=blk(T.xl, j), op=add).then_inc(S["os%d" % j], 1)
+        g.wait_ge(S["os%d" % j], 1)
+        s = slot[(rank, mine[j])]
+        send(cores[mine[j]], blk(T.al, s), blk(T.out, j), S["ar%d" % s], off_mask)
+
+    v.wait_ge(S.x2, n_on)
+    v.tensor_tensor(out=blk(T.acc, 0), in0=blk(T.m, 3), in1=T.xl2[:, :], op=add).then_inc(S.vq, 1)
+    nv[0] += 1
+    for s in range(3):
+        v.wait_ge(S["ar%d" % s], n_off)
+        v.wait_ge(S.vq, nv[0])
+        ins = v.tensor_tensor(out=blk(T.acc, s + 1), in0=blk(T.acc, s), in1=blk(T.al, s), op=add)
+        if s < 2:
+            ins.then_inc(S.vq, 1)
+            nv[0] += 1
+        else:
+            ins.then_inc(S.sacc, 1)
+
+    g.sync.wait_ge(S.sacc, 1)
+    g.sync.dma_start(out=T.y[:, :], in_=blk(T.acc, 3)).then_inc(S.stored, 16)
+    g.wait_ge(S.sent, sent[0])
+    g.wait_ge(S.stored, 16)

@@ -7,165 +7,203 @@ W = NB * F
 
 SCRATCH = {
     "tab": ("sbuf", [128, KT * W], "bfloat16"),
-    "u": ("sbuf", [128, W], "float32"),
-    "st": ("sbuf", [128, 3 * F], "float32"),
+    "raws": ("sbuf", [128, F], "bfloat16"),
+    "ph": ("psum", [128, 4 * F], "float32"),
+    "pc": ("psum", [128, 4 * F], "float32"),
+    "pp": ("psum", [128, 4 * F], "float32"),
+    "pm": ("psum", [128, 4 * F], "float32"),
+    "pm2": ("psum", [128, 4 * F], "float32"),
+    "pa": ("psum", [128, 4 * F], "float32"),
+    "sth": ("sbuf", [128, 2 * F], "float32"),
+    "st": ("sbuf", [128, 2 * F], "float32"),
     "st2": ("sbuf", [128, F], "float32"),
-    "m": ("sbuf", [128, 4 * F], "float32"),
-    "m2": ("sbuf", [128, F], "float32"),
+    "hl": ("sbuf", [128, 4 * F], "float32"),
     "rawl": ("sbuf", [128, F], "bfloat16"),
-    "xl": ("sbuf", [128, 3 * F], "float32"),
+    "xl": ("sbuf", [128, 2 * F], "float32"),
     "xl2": ("sbuf", [128, F], "float32"),
-    "out": ("sbuf", [128, 3 * F], "float32"),
+    "out": ("sbuf", [128, 2 * F], "float32"),
     "al": ("sbuf", [128, 3 * F], "float32"),
-    "acc": ("sbuf", [128, 4 * F], "float32"),
+    "acc": ("sbuf", [128, F], "float32"),
 }
-SEMAPHORES = ["lc0", "lc1", "lc2", "lr0", "lr1", "lr2", "vq", "sst", "sst2", "xraw", "x1", "x2",
-              "os0", "os1", "os2", "ar0", "ar1", "ar2", "sacc", "stored", "sent"]
+SEMAPHORES = (["lraw"] + ["l%d%d" % (i, k) for i in range(4) for k in range(KT)]
+              + ["vq", "ssh0", "ssh1", "sst", "sst2", "h00", "h01", "h10", "h11", "xraw", "x1", "x2",
+                 "os0", "os1", "ar0", "ar1", "ar2", "sacc", "stored", "sent"])
 
 
-def _runs(blocks):
-    res = []
-    for pos, b in enumerate(blocks):
-        if res and res[-1][0] + res[-1][1] == b:
-            res[-1][1] += 1
-        else:
-            res.append([b, 1, pos])
-    return res
+def _ones(mask):
+    return bin(mask).count("1")
 
 
 def _plan(T, topo):
     cores = list(T.cores)
-    n = len(cores)
-    bychip = {}
+    chips, members = [], {}
     for r, c in enumerate(cores):
-        bychip.setdefault(topo.chip(c), []).append(r)
-    info = {}
-    for ch, (ra, rb) in bychip.items():
-        off = [r for r in range(n) if r not in (ra, rb)]
-        lo, hi = off[:len(off) // 2], off[len(off) // 2:]
-        if hi[0] > rb:
-            three, five, p3, p5 = hi, lo, (hi[0], n), (0, hi[0])
-        else:
-            three, five, p3, p5 = lo, hi, (0, lo[-1] + 1), (lo[-1] + 1, n)
-        info[ra] = dict(peer=rb, mine=three, theirs=five, crit=p5, rest=p3)
-        info[rb] = dict(peer=ra, mine=five, theirs=three, crit=p3, rest=p5)
-    arrivals = {d: [] for d in range(n)}
-    for r in range(n):
-        me = topo.chip(cores[r])
-        mine = info[r]["mine"]
-        order = sorted(range(len(mine)), key=lambda j: (topo.same_plane(me, topo.chip(cores[mine[j]])), mine[j]))
-        info[r]["order"] = order
-        for pos, j in enumerate(order):
-            arrivals[mine[j]].append((pos, r))
-    slot = {}
-    for d in range(n):
-        for s, (pos, r) in enumerate(sorted(arrivals[d])):
+        ch = topo.chip(c)
+        if ch not in members:
+            members[ch] = []
+            chips.append(ch)
+        members[ch].append(r)
+    info, helpers = {}, {}
+    for ch in chips:
+        ra, rb = members[ch]
+        plane = [o for o in chips if topo.same_plane(ch, o)]
+        cross = [o for o in chips if o != ch and not topo.same_plane(ch, o)]
+        hb = list(members[plane[0]])
+        hc = [x for x in range(topo.CHIPS * topo.CORES_PER_CHIP)
+              if topo.chip(x) == ch and T.rank_of(x) is None and topo.die(x) != topo.die(cores[ra])
+              and all(topo.may_write(x, cores[d]) for d in hb)][0]
+        hmask = topo.mask(hc, cores[hb[0]]) & topo.mask(hc, cores[hb[1]])
+        helpers[hc] = dict(ranks=(ra, rb), blocks=hb, mask=hmask)
+        for pos, (r, o) in enumerate(((ra, cross[0]), (rb, cross[1]))):
+            back = [q for q in chips if q != o and not topo.same_plane(o, q)]
+            grp = list(members[o])
+            seq = grp if back.index(ch) == 0 else grp[::-1]
+            off = topo.mask(cores[r], cores[seq[0]]) & topo.mask(cores[r], cores[seq[1]])
+            info[r] = dict(peer=(rb if r == ra else ra), pos=pos, seq=seq, hblocks=hb, helper=hc, off=off)
+    arrivals = {d: [] for d in range(len(cores))}
+    for r in info:
+        for rnd, b in enumerate(info[r]["seq"]):
+            arrivals[b].append((rnd, r))
+    slot, need = {}, {}
+    for d in arrivals:
+        for s, (rnd, r) in enumerate(sorted(arrivals[d])):
             slot[(r, d)] = s
-    return info, slot
+            need[(d, s)] = _ones(info[r]["off"])
+    for hc in helpers:
+        for d in helpers[hc]["blocks"]:
+            need[(d, 2)] = _ones(helpers[hc]["mask"])
+    return info, helpers, slot, need
 
 
 def rank_program(g, core, T, topo):
-    rank = T.rank_of(core)
-    if rank is None:
-        return
     cores = list(T.cores)
-    info, slot = _plan(T, topo)
-    me = info[rank]
-    peer, mine, theirs, order = me["peer"], me["mine"], me["theirs"], me["order"]
-    pcore = cores[peer]
+    info, helpers, slot, need = _plan(T, topo)
+    rank = T.rank_of(core)
+    if rank is None and core not in helpers:
+        return
     S = T.sem
     add = AluOpType.add
     v = g.vector
-
-    def tab(k, b, nb=1):
-        return T.tab[:, k * W + b * F: k * W + (b + nb) * F]
+    sent = [0]
+    nv = [0]
 
     def blk(buf, pos, nb=1):
         return buf[:, pos * F:(pos + nb) * F]
-
-    (c0, c1), (r0, r1) = me["crit"], me["rest"]
-    jobs = [(g.sync, 0, c0, c1, S.lc0), (g.scalar, 1, c0, c1, S.lc1), (g.sync, 2, c0, c1, S.lc2),
-            (g.scalar, 0, r0, r1, S.lr0), (g.sync, 1, r0, r1, S.lr1), (g.scalar, 2, r0, r1, S.lr2)]
-    for q, k, b0, b1, sem in jobs:
-        q.dma_start(out=tab(k, b0, b1 - b0), in_=T.gr[k, :, b0 * F:b1 * F]).then_inc(sem, 16)
-
-    off_mask = topo.mask(core, cores[mine[0]])
-    for d in mine:
-        off_mask &= topo.mask(core, cores[d])
-    on_mask = topo.mask(core, pcore) & off_mask
-    n_on = bin(on_mask).count("1")
-    n_off = bin(off_mask).count("1")
-    sent = [0]
 
     def send(dst_core, out_ap, in_ap, sem, mask):
         assert topo.may_write(core, dst_core)
         rid, pid, _se = topo.addr(dst_core)
         g.remote_dma(out_ap=out_ap, in_ap=in_ap, remote_sem=sem, local_sem=S.sent, pid=pid, routing_id=rid,
                      dma_engine_mask=mask)
-        sent[0] += bin(mask).count("1")
+        sent[0] += _ones(mask)
 
-    g.wait_ge(S.lc0, 16)
-    send(pcore, T.rawl[:, :], tab(0, theirs[0]), S.xraw, on_mask)
-
-    nv = [0]
-    late = _runs(theirs[1:])
-    v.wait_ge(S.lc0, 16)
-    v.wait_ge(S.lc1, 16)
-    for b, nb, pos in late:
-        v.tensor_tensor(out=blk(T.u, b, nb), in0=tab(0, b, nb), in1=tab(1, b, nb), op=add).then_inc(S.vq, 1)
-        nv[0] += 1
-    v.wait_ge(S.lc2, 16)
-    v.tensor_tensor(out=blk(T.st, 0), in0=tab(1, theirs[0]), in1=tab(2, theirs[0]), op=add).then_inc(S.sst, 1)
-    v.wait_ge(S.vq, nv[0])
-    for b, nb, pos in late:
-        v.tensor_tensor(out=blk(T.st, pos + 1, nb), in0=blk(T.u, b, nb), in1=tab(2, b, nb), op=add).then_inc(S.sst, 1)
-    g.wait_ge(S.sst, 1 + len(late))
-    send(pcore, T.xl[:, :], T.st[:, :], S.x1, on_mask)
-
-    rem = _runs(sorted(mine + [rank, peer]))
-    v.wait_ge(S.lr0, 16)
-    v.wait_ge(S.lr1, 16)
-    for b, nb, pos in rem:
-        v.tensor_tensor(out=blk(T.u, b, nb), in0=tab(0, b, nb), in1=tab(1, b, nb), op=add).then_inc(S.vq, 1)
-        nv[0] += 1
-    v.wait_ge(S.lr2, 16)
-    v.wait_ge(S.vq, nv[0])
-    v.tensor_tensor(out=T.st2[:, :], in0=blk(T.u, peer), in1=tab(2, peer), op=add).then_inc(S.sst2, 1)
-    g.wait_ge(S.sst2, 1)
-    send(pcore, T.xl2[:, :], T.st2[:, :], S.x2, on_mask)
-    for b, nb, pos in _runs(mine):
-        v.tensor_tensor(out=blk(T.m, pos, nb), in0=blk(T.u, b, nb), in1=tab(2, b, nb), op=add).then_inc(S.vq, 1)
-        nv[0] += 1
-    v.tensor_tensor(out=blk(T.m, 3), in0=blk(T.u, rank), in1=tab(2, rank), op=add).then_inc(S.vq, 1)
-    nv[0] += 1
-
-    v.wait_ge(S.xraw, n_on)
-    v.wait_ge(S.vq, nv[0])
-    v.tensor_tensor(out=T.m2[:, :], in0=blk(T.m, 0), in1=T.rawl[:, :], op=add).then_inc(S.vq, 1)
-    nv[0] += 1
-    v.wait_ge(S.x1, n_on)
-    v.wait_ge(S.vq, nv[0])
-    for j in order:
-        src = T.m2[:, :] if j == 0 else blk(T.m, j)
-        v.tensor_tensor(out=blk(T.out, j), in0=src, in1=blk(T.xl, j), op=add).then_inc(S["os%d" % j], 1)
-        g.wait_ge(S["os%d" % j], 1)
-        s = slot[(rank, mine[j])]
-        send(cores[mine[j]], blk(T.al, s), blk(T.out, j), S["ar%d" % s], off_mask)
-
-    v.wait_ge(S.x2, n_on)
-    v.tensor_tensor(out=blk(T.acc, 0), in0=blk(T.m, 3), in1=T.xl2[:, :], op=add).then_inc(S.vq, 1)
-    nv[0] += 1
-    for s in range(3):
-        v.wait_ge(S["ar%d" % s], n_off)
-        v.wait_ge(S.vq, nv[0])
-        ins = v.tensor_tensor(out=blk(T.acc, s + 1), in0=blk(T.acc, s), in1=blk(T.al, s), op=add)
-        if s < 2:
+    def vadd(out, in0, in1, sem=None):
+        ins = v.tensor_tensor(out=out, in0=in0, in1=in1, op=add)
+        if sem is None:
             ins.then_inc(S.vq, 1)
             nv[0] += 1
         else:
-            ins.then_inc(S.sacc, 1)
+            ins.then_inc(sem, 1)
+
+    if rank is None:
+        hi = helpers[core]
+        for p, d in enumerate(hi["blocks"]):
+            for pos, r in enumerate(hi["ranks"]):
+                v.wait_ge(S["h%d%d" % (pos, p)], _ones(topo.mask(cores[r], core) & info[r]["off"]))
+            vadd(blk(T.out, p), blk(T.hl, p), blk(T.hl, 2 + p), S["os%d" % p])
+            g.wait_ge(S["os%d" % p], 1)
+            send(cores[d], blk(T.al, 2), blk(T.out, p), S.ar2, hi["mask"])
+        g.wait_ge(S.sent, sent[0])
+        return
+
+    me = info[rank]
+    peer, seq, hb, hcore, pos_me = me["peer"], me["seq"], me["hblocks"], me["helper"], me["pos"]
+    pseq = info[peer]["seq"]
+    pcore = cores[peer]
+
+    def tab(k, b, nb=1):
+        return T.tab[:, k * W + b * F: k * W + (b + nb) * F]
+
+    g.sync.dma_start(out=T.raws[:, :], in_=T.gr[0, :, pseq[0] * F:(pseq[0] + 1) * F]).then_inc(S.lraw, 16)
+    queues = [g.scalar, g.sync]
+    nq = 0
+    for i, b0 in enumerate((min(hb), min(pseq), min(seq), min(rank, peer))):
+        for k in range(KT):
+            queues[nq % 2].dma_start(out=tab(k, b0, 2), in_=T.gr[k, :, b0 * F:(b0 + 2) * F]).then_inc(S["l%d%d" % (i, k)], 16)
+            nq += 1
+
+    off_mask = me["off"]
+    on_mask = topo.mask(core, pcore) & off_mask
+    h_mask = topo.mask(core, hcore) & off_mask
+    n_on = _ones(on_mask)
+
+    g.wait_ge(S.lraw, 16)
+    send(pcore, T.rawl[:, :], T.raws[:, :], S.xraw, on_mask)
+
+    v.wait_ge(S.l00, 16)
+    v.wait_ge(S.l01, 16)
+    vadd(blk(T.ph, 0, 2), tab(0, hb[0], 2), tab(1, hb[0], 2))
+    v.wait_ge(S.l11, 16)
+    v.tensor_copy(out=blk(T.pc, 0), in_=tab(1, pseq[0])).then_inc(S.vq, 1)
+    nv[0] += 1
+    v.wait_ge(S.l10, 16)
+    vadd(blk(T.pc, 1), tab(0, pseq[1]), tab(1, pseq[1]))
+    v.wait_ge(S.l02, 16)
+    v.wait_ge(S.vq, nv[0])
+    vadd(blk(T.sth, 0), blk(T.ph, 0), tab(2, hb[0]), S.ssh0)
+    vadd(blk(T.sth, 1), blk(T.ph, 1), tab(2, hb[1]), S.ssh1)
+    v.wait_ge(S.l12, 16)
+    for p in range(2):
+        vadd(blk(T.st, p), blk(T.pc, p), tab(2, pseq[p]), S.sst)
+    g.wait_ge(S.ssh0, 1)
+    send(hcore, blk(T.hl, 2 * pos_me), blk(T.sth, 0), S["h%d0" % pos_me], h_mask)
+    g.wait_ge(S.sst, 2)
+    send(pcore, T.xl[:, :], T.st[:, :], S.x1, on_mask)
+    g.wait_ge(S.ssh1, 1)
+    send(hcore, blk(T.hl, 2 * pos_me + 1), blk(T.sth, 1), S["h%d1" % pos_me], h_mask)
+
+    v.wait_ge(S.l20, 16)
+    v.wait_ge(S.l21, 16)
+    for p in range(2):
+        vadd(blk(T.pm, p), tab(0, seq[p]), tab(1, seq[p]))
+    v.wait_ge(S.l30, 16)
+    v.wait_ge(S.l31, 16)
+    vadd(blk(T.pp, 0), tab(0, peer), tab(1, peer))
+    v.wait_ge(S.l22, 16)
+    v.wait_ge(S.vq, nv[0])
+    for p in range(2):
+        vadd(blk(T.pm2, p), blk(T.pm, p), tab(2, seq[p]))
+    v.wait_ge(S.l32, 16)
+    vadd(T.st2[:, :], blk(T.pp, 0), tab(2, peer), S.sst2)
+    g.wait_ge(S.sst2, 1)
+    send(pcore, T.xl2[:, :], T.st2[:, :], S.x2, on_mask)
+
+    v.wait_ge(S.xraw, n_on)
+    v.wait_ge(S.vq, nv[0])
+    vadd(blk(T.pm2, 3), blk(T.pm2, 0), T.rawl[:, :])
+    v.wait_ge(S.x1, n_on)
+    v.wait_ge(S.vq, nv[0])
+    for p in range(2):
+        vadd(blk(T.out, p), blk(T.pm2, 3 if p == 0 else p), blk(T.xl, p), S["os%d" % p])
+        g.wait_ge(S["os%d" % p], 1)
+        s = slot[(rank, seq[p])]
+        send(cores[seq[p]], blk(T.al, s), blk(T.out, p), S["ar%d" % s], off_mask)
+
+    vadd(blk(T.pm, 3), tab(0, rank), tab(1, rank))
+    v.wait_ge(S.vq, nv[0])
+    vadd(blk(T.pa, 0), blk(T.pm, 3), tab(2, rank))
+    v.wait_ge(S.x2, n_on)
+    v.wait_ge(S.vq, nv[0])
+    vadd(blk(T.pa, 1), blk(T.pa, 0), T.xl2[:, :])
+    for s in range(3):
+        v.wait_ge(S["ar%d" % s], need[(rank, s)])
+        v.wait_ge(S.vq, nv[0])
+        if s < 2:
+            vadd(blk(T.pa, s + 2), blk(T.pa, s + 1), blk(T.al, s))
+        else:
+            vadd(T.acc[:, :], blk(T.pa, s + 1), blk(T.al, s), S.sacc)
 
     g.sync.wait_ge(S.sacc, 1)
-    g.sync.dma_start(out=T.y[:, :], in_=blk(T.acc, 3)).then_inc(S.stored, 16)
+    g.sync.dma_start(out=T.y[:, :], in_=T.acc[:, :]).then_inc(S.stored, 16)
     g.wait_ge(S.sent, sent[0])
     g.wait_ge(S.stored, 16)

@@ -8,11 +8,14 @@ W = NB * F
 SCRATCH = {
     "tab": ("sbuf", [128, KT * W], "bfloat16"),
     "raws": ("sbuf", [128, F], "bfloat16"),
+    "ones": ("sbuf", [128, F], "bfloat16"),
+    "idn": ("sbuf", [128, F], "bfloat16"),
     "ph": ("psum", [128, 4 * F], "float32"),
     "pc": ("psum", [128, 4 * F], "float32"),
+    "pm0": ("psum", [128, 4 * F], "float32"),
+    "pm1": ("psum", [128, 4 * F], "float32"),
     "pp": ("psum", [128, 4 * F], "float32"),
-    "pm": ("psum", [128, 4 * F], "float32"),
-    "pm2": ("psum", [128, 4 * F], "float32"),
+    "po": ("psum", [128, 4 * F], "float32"),
     "pa": ("psum", [128, 4 * F], "float32"),
     "sth": ("sbuf", [128, 2 * F], "float32"),
     "st": ("sbuf", [128, 2 * F], "float32"),
@@ -25,8 +28,9 @@ SCRATCH = {
     "al": ("sbuf", [128, 3 * F], "float32"),
     "acc": ("sbuf", [128, F], "float32"),
 }
-SEMAPHORES = (["lraw"] + ["l%d%d" % (i, k) for i in range(4) for k in range(KT)]
-              + ["vq", "ssh0", "ssh1", "sst", "sst2", "h00", "h01", "h10", "h11", "xraw", "x1", "x2",
+SEMAPHORES = (["lraw"] + ["l%s%d" % (i, k) for i in "chmo" for k in range(KT)]
+              + ["sone", "sid", "tph", "tpc", "tpm0", "tpm1", "tpp", "tpo",
+                 "vq", "ssh0", "ssh1", "sst", "sst2", "h00", "h01", "h10", "h11", "xraw", "x1", "x2",
                  "os0", "os1", "ar0", "ar1", "ar2", "sacc", "stored", "sent"])
 
 
@@ -84,6 +88,7 @@ def rank_program(g, core, T, topo):
     S = T.sem
     add = AluOpType.add
     v = g.vector
+    te = g.tensor
     sent = [0]
     nv = [0]
 
@@ -109,7 +114,7 @@ def rank_program(g, core, T, topo):
         hi = helpers[core]
         for p, d in enumerate(hi["blocks"]):
             for pos, r in enumerate(hi["ranks"]):
-                v.wait_ge(S["h%d%d" % (pos, p)], _ones(topo.mask(cores[r], core) & info[r]["off"]))
+                v.wait_ge(S["h%d%d" % (pos, p)], _ones(topo.mask(cores[r], core)))
             vadd(blk(T.out, p), blk(T.hl, p), blk(T.hl, 2 + p), S["os%d" % p])
             g.wait_ge(S["os%d" % p], 1)
             send(cores[d], blk(T.al, 2), blk(T.out, p), S.ar2, hi["mask"])
@@ -124,84 +129,99 @@ def rank_program(g, core, T, topo):
     def tab(k, b, nb=1):
         return T.tab[:, k * W + b * F: k * W + (b + nb) * F]
 
+    def mm(out, rhs, start, stop, sem=None):
+        ins = te.matmul(out, T.idn[:, :], rhs, start, stop)
+        if sem is not None:
+            ins.then_inc(sem, 1)
+
     g.sync.dma_start(out=T.raws[:, :], in_=T.gr[0, :, pseq[0] * F:(pseq[0] + 1) * F]).then_inc(S.lraw, 16)
     queues = [g.scalar, g.sync]
     nq = 0
-    for i, b0 in enumerate((min(hb), min(pseq), min(seq), min(rank, peer))):
+    for i, b0 in (("c", min(pseq)), ("h", min(hb)), ("m", min(seq)), ("o", min(rank, peer))):
         for k in range(KT):
-            queues[nq % 2].dma_start(out=tab(k, b0, 2), in_=T.gr[k, :, b0 * F:(b0 + 2) * F]).then_inc(S["l%d%d" % (i, k)], 16)
+            queues[nq % 2].dma_start(out=tab(k, b0, 2), in_=T.gr[k, :, b0 * F:(b0 + 2) * F]).then_inc(S["l%s%d" % (i, k)], 16)
             nq += 1
 
     off_mask = me["off"]
-    on_mask = topo.mask(core, pcore) & off_mask
-    h_mask = topo.mask(core, hcore) & off_mask
+    on_mask = topo.mask(core, pcore)
+    h_mask = topo.mask(core, hcore)
     n_on = _ones(on_mask)
+
+    v.memset(T.ones[:, :], 1.0).then_inc(S.sone, 1)
+    g.wait_ge(S.sone, 1)
+    g.affine_select(T.idn[:, :], T.ones[:, :], [[-1, F]], AluOpType.is_equal, 0.0, 0, 1).then_inc(S.sid, 1)
+
+    te.wait_ge(S.sid, 1)
+    te.wait_ge(S.lc0, 16)
+    mm(blk(T.pc, 1), tab(0, pseq[1]), True, False)
+    te.wait_ge(S.lc1, 16)
+    mm(blk(T.pc, 1), tab(1, pseq[1]), False, True, S.tpc)
+    mm(blk(T.pc, 0), tab(1, pseq[0]), True, True, S.tpc)
+    te.wait_ge(S.lh0, 16)
+    mm(blk(T.ph, 0, 2), tab(0, hb[0], 2), True, False)
+    te.wait_ge(S.lh1, 16)
+    mm(blk(T.ph, 0, 2), tab(1, hb[0], 2), False, True, S.tph)
+    te.wait_ge(S.lm0, 16)
+    mm(blk(T.pm0, 0), tab(0, seq[0]), True, False)
+    mm(blk(T.pm1, 0), tab(0, seq[1]), True, False)
+    te.wait_ge(S.xraw, n_on)
+    mm(blk(T.pm0, 0), T.rawl[:, :], False, False)
+    te.wait_ge(S.lm1, 16)
+    mm(blk(T.pm0, 0), tab(1, seq[0]), False, False)
+    mm(blk(T.pm1, 0), tab(1, seq[1]), False, False)
+    te.wait_ge(S.lm2, 16)
+    mm(blk(T.pm0, 0), tab(2, seq[0]), False, True, S.tpm0)
+    mm(blk(T.pm1, 0), tab(2, seq[1]), False, True, S.tpm1)
+    te.wait_ge(S.lo0, 16)
+    mm(blk(T.pp, 0), tab(0, peer), True, False)
+    mm(blk(T.po, 0), tab(0, rank), True, False)
+    te.wait_ge(S.lo1, 16)
+    mm(blk(T.pp, 0), tab(1, peer), False, True, S.tpp)
+    mm(blk(T.po, 0), tab(1, rank), False, False)
+    te.wait_ge(S.lo2, 16)
+    mm(blk(T.po, 0), tab(2, rank), False, True, S.tpo)
 
     g.wait_ge(S.lraw, 16)
     send(pcore, T.rawl[:, :], T.raws[:, :], S.xraw, on_mask)
 
-    v.wait_ge(S.l00, 16)
-    v.wait_ge(S.l01, 16)
-    vadd(blk(T.ph, 0, 2), tab(0, hb[0], 2), tab(1, hb[0], 2))
-    v.wait_ge(S.l11, 16)
-    v.tensor_copy(out=blk(T.pc, 0), in_=tab(1, pseq[0])).then_inc(S.vq, 1)
-    nv[0] += 1
-    v.wait_ge(S.l10, 16)
-    vadd(blk(T.pc, 1), tab(0, pseq[1]), tab(1, pseq[1]))
-    v.wait_ge(S.l02, 16)
-    v.wait_ge(S.vq, nv[0])
-    vadd(blk(T.sth, 0), blk(T.ph, 0), tab(2, hb[0]), S.ssh0)
-    vadd(blk(T.sth, 1), blk(T.ph, 1), tab(2, hb[1]), S.ssh1)
-    v.wait_ge(S.l12, 16)
+    v.wait_ge(S.tpc, 2)
+    v.wait_ge(S.lc2, 16)
     for p in range(2):
         vadd(blk(T.st, p), blk(T.pc, p), tab(2, pseq[p]), S.sst)
-    g.wait_ge(S.ssh0, 1)
-    send(hcore, blk(T.hl, 2 * pos_me), blk(T.sth, 0), S["h%d0" % pos_me], h_mask)
     g.wait_ge(S.sst, 2)
     send(pcore, T.xl[:, :], T.st[:, :], S.x1, on_mask)
-    g.wait_ge(S.ssh1, 1)
-    send(hcore, blk(T.hl, 2 * pos_me + 1), blk(T.sth, 1), S["h%d1" % pos_me], h_mask)
 
-    v.wait_ge(S.l20, 16)
-    v.wait_ge(S.l21, 16)
+    v.wait_ge(S.tph, 1)
+    v.wait_ge(S.lh2, 16)
     for p in range(2):
-        vadd(blk(T.pm, p), tab(0, seq[p]), tab(1, seq[p]))
-    v.wait_ge(S.l30, 16)
-    v.wait_ge(S.l31, 16)
-    vadd(blk(T.pp, 0), tab(0, peer), tab(1, peer))
-    v.wait_ge(S.l22, 16)
-    v.wait_ge(S.vq, nv[0])
-    for p in range(2):
-        vadd(blk(T.pm2, p), blk(T.pm, p), tab(2, seq[p]))
-    v.wait_ge(S.l32, 16)
-    vadd(T.st2[:, :], blk(T.pp, 0), tab(2, peer), S.sst2)
-    g.wait_ge(S.sst2, 1)
-    send(pcore, T.xl2[:, :], T.st2[:, :], S.x2, on_mask)
+        vadd(blk(T.sth, p), blk(T.ph, p), tab(2, hb[p]), S["ssh%d" % p])
+        g.wait_ge(S["ssh%d" % p], 1)
+        send(hcore, blk(T.hl, 2 * pos_me + p), blk(T.sth, p), S["h%d%d" % (pos_me, p)], h_mask)
 
-    v.wait_ge(S.xraw, n_on)
-    v.wait_ge(S.vq, nv[0])
-    vadd(blk(T.pm2, 3), blk(T.pm2, 0), T.rawl[:, :])
     v.wait_ge(S.x1, n_on)
-    v.wait_ge(S.vq, nv[0])
     for p in range(2):
-        vadd(blk(T.out, p), blk(T.pm2, 3 if p == 0 else p), blk(T.xl, p), S["os%d" % p])
+        v.wait_ge(S["tpm%d" % p], 1)
+        vadd(blk(T.out, p), blk(T["pm%d" % p], 0), blk(T.xl, p), S["os%d" % p])
         g.wait_ge(S["os%d" % p], 1)
         s = slot[(rank, seq[p])]
         send(cores[seq[p]], blk(T.al, s), blk(T.out, p), S["ar%d" % s], off_mask)
 
-    vadd(blk(T.pm, 3), tab(0, rank), tab(1, rank))
-    v.wait_ge(S.vq, nv[0])
-    vadd(blk(T.pa, 0), blk(T.pm, 3), tab(2, rank))
+    v.wait_ge(S.tpp, 1)
+    v.wait_ge(S.lo2, 16)
+    vadd(T.st2[:, :], blk(T.pp, 0), tab(2, peer), S.sst2)
+    g.wait_ge(S.sst2, 1)
+    send(pcore, T.xl2[:, :], T.st2[:, :], S.x2, on_mask)
+
+    v.wait_ge(S.tpo, 1)
     v.wait_ge(S.x2, n_on)
-    v.wait_ge(S.vq, nv[0])
-    vadd(blk(T.pa, 1), blk(T.pa, 0), T.xl2[:, :])
+    vadd(blk(T.pa, 0), blk(T.po, 0), T.xl2[:, :])
     for s in range(3):
         v.wait_ge(S["ar%d" % s], need[(rank, s)])
         v.wait_ge(S.vq, nv[0])
         if s < 2:
-            vadd(blk(T.pa, s + 2), blk(T.pa, s + 1), blk(T.al, s))
+            vadd(blk(T.pa, s + 1), blk(T.pa, s), blk(T.al, s))
         else:
-            vadd(T.acc[:, :], blk(T.pa, s + 1), blk(T.al, s), S.sacc)
+            vadd(T.acc[:, :], blk(T.pa, s), blk(T.al, s), S.sacc)
 
     g.sync.wait_ge(S.sacc, 1)
     g.sync.dma_start(out=T.y[:, :], in_=T.acc[:, :]).then_inc(S.stored, 16)

from concourse.mybir import AluOpType

F = 128
KT = 3
NB = 8
W = NB * F

SCRATCH = {
    "tab": ("sbuf", [128, KT * W], "bfloat16"),
    "raws": ("sbuf", [128, F], "bfloat16"),
    "ones": ("sbuf", [128, F], "bfloat16"),
    "idn": ("sbuf", [128, F], "bfloat16"),
    "ph": ("psum", [128, 4 * F], "float32"),
    "pc": ("psum", [128, 4 * F], "float32"),
    "pm0": ("psum", [128, 4 * F], "float32"),
    "pm1": ("psum", [128, 4 * F], "float32"),
    "pp": ("psum", [128, 4 * F], "float32"),
    "po": ("psum", [128, 4 * F], "float32"),
    "pa": ("psum", [128, 4 * F], "float32"),
    "sth": ("sbuf", [128, 2 * F], "float32"),
    "st": ("sbuf", [128, 2 * F], "float32"),
    "st2": ("sbuf", [128, F], "float32"),
    "hl": ("sbuf", [128, 4 * F], "float32"),
    "rawl": ("sbuf", [128, F], "bfloat16"),
    "xl": ("sbuf", [128, 2 * F], "float32"),
    "xl2": ("sbuf", [128, F], "float32"),
    "out": ("sbuf", [128, 2 * F], "float32"),
    "al": ("sbuf", [128, 3 * F], "float32"),
    "acc": ("sbuf", [128, F], "float32"),
}
SEMAPHORES = (["lraw"] + ["l%s%d" % (i, k) for i in "chmo" for k in range(KT)]
              + ["sone", "sid", "tph", "tpc", "tpm0", "tpm1", "tpp", "tpo",
                 "vq", "ssh0", "ssh1", "sst", "sst2", "h00", "h01", "h10", "h11", "xraw", "x1", "x2",
                 "os0", "os1", "ar0", "ar1", "ar2", "sacc", "stored", "sent"])


def _ones(mask):
    return bin(mask).count("1")


def _plan(T, topo):
    cores = list(T.cores)
    chips, members = [], {}
    for r, c in enumerate(cores):
        ch = topo.chip(c)
        if ch not in members:
            members[ch] = []
            chips.append(ch)
        members[ch].append(r)
    info, helpers = {}, {}
    for ch in chips:
        ra, rb = members[ch]
        plane = [o for o in chips if topo.same_plane(ch, o)]
        cross = [o for o in chips if o != ch and not topo.same_plane(ch, o)]
        hb = list(members[plane[0]])
        hc = [x for x in range(topo.CHIPS * topo.CORES_PER_CHIP)
              if topo.chip(x) == ch and T.rank_of(x) is None and topo.die(x) != topo.die(cores[ra])
              and all(topo.may_write(x, cores[d]) for d in hb)][0]
        hmask = topo.mask(hc, cores[hb[0]]) & topo.mask(hc, cores[hb[1]])
        helpers[hc] = dict(ranks=(ra, rb), blocks=hb, mask=hmask)
        for pos, (r, o) in enumerate(((ra, cross[0]), (rb, cross[1]))):
            back = [q for q in chips if q != o and not topo.same_plane(o, q)]
            grp = list(members[o])
            seq = grp if back.index(ch) == 0 else grp[::-1]
            off = topo.mask(cores[r], cores[seq[0]]) & topo.mask(cores[r], cores[seq[1]])
            info[r] = dict(peer=(rb if r == ra else ra), pos=pos, seq=seq, hblocks=hb, helper=hc, off=off)
    arrivals = {d: [] for d in range(len(cores))}
    for r in info:
        for rnd, b in enumerate(info[r]["seq"]):
            arrivals[b].append((rnd, r))
    slot, need = {}, {}
    for d in arrivals:
        for s, (rnd, r) in enumerate(sorted(arrivals[d])):
            slot[(r, d)] = s
            need[(d, s)] = _ones(info[r]["off"])
    for hc in helpers:
        for d in helpers[hc]["blocks"]:
            need[(d, 2)] = _ones(helpers[hc]["mask"])
    return info, helpers, slot, need


def rank_program(g, core, T, topo):
    cores = list(T.cores)
    info, helpers, slot, need = _plan(T, topo)
    rank = T.rank_of(core)
    if rank is None and core not in helpers:
        return
    S = T.sem
    add = AluOpType.add
    v = g.vector
    te = g.tensor
    sent = [0]
    nv = [0]

    def blk(buf, pos, nb=1):
        return buf[:, pos * F:(pos + nb) * F]

    def send(dst_core, out_ap, in_ap, sem, mask):
        assert topo.may_write(core, dst_core)
        rid, pid, _se = topo.addr(dst_core)
        g.remote_dma(out_ap=out_ap, in_ap=in_ap, remote_sem=sem, local_sem=S.sent, pid=pid, routing_id=rid,
                     dma_engine_mask=mask)
        sent[0] += _ones(mask)

    def vadd(out, in0, in1, sem=None):
        ins = v.tensor_tensor(out=out, in0=in0, in1=in1, op=add)
        if sem is None:
            ins.then_inc(S.vq, 1)
            nv[0] += 1
        else:
            ins.then_inc(sem, 1)

    if rank is None:
        hi = helpers[core]
        for p, d in enumerate(hi["blocks"]):
            for pos, r in enumerate(hi["ranks"]):
                v.wait_ge(S["h%d%d" % (pos, p)], _ones(topo.mask(cores[r], core)))
            vadd(blk(T.out, p), blk(T.hl, p), blk(T.hl, 2 + p), S["os%d" % p])
            g.wait_ge(S["os%d" % p], 1)
            send(cores[d], blk(T.al, 2), blk(T.out, p), S.ar2, hi["mask"])
        g.wait_ge(S.sent, sent[0])
        return

    me = info[rank]
    peer, seq, hb, hcore, pos_me = me["peer"], me["seq"], me["hblocks"], me["helper"], me["pos"]
    pseq = info[peer]["seq"]
    pcore = cores[peer]

    def tab(k, b, nb=1):
        return T.tab[:, k * W + b * F: k * W + (b + nb) * F]

    def mm(out, rhs, start, stop, sem=None):
        ins = te.matmul(out, T.idn[:, :], rhs, start, stop)
        if sem is not None:
            ins.then_inc(sem, 1)

    g.sync.dma_start(out=T.raws[:, :], in_=T.gr[0, :, pseq[0] * F:(pseq[0] + 1) * F]).then_inc(S.lraw, 16)
    queues = [g.scalar, g.sync]
    nq = 0
    for i, b0 in (("c", min(pseq)), ("h", min(hb)), ("m", min(seq)), ("o", min(rank, peer))):
        for k in range(KT):
            queues[nq % 2].dma_start(out=tab(k, b0, 2), in_=T.gr[k, :, b0 * F:(b0 + 2) * F]).then_inc(S["l%s%d" % (i, k)], 16)
            nq += 1

    off_mask = me["off"]
    on_mask = topo.mask(core, pcore)
    h_mask = topo.mask(core, hcore)
    n_on = _ones(on_mask)

    v.memset(T.ones[:, :], 1.0).then_inc(S.sone, 1)
    g.wait_ge(S.sone, 1)
    g.affine_select(T.idn[:, :], T.ones[:, :], [[-1, F]], AluOpType.is_equal, 0.0, 0, 1).then_inc(S.sid, 1)

    te.wait_ge(S.sid, 1)
    te.wait_ge(S.lc0, 16)
    mm(blk(T.pc, 1), tab(0, pseq[1]), True, False)
    te.wait_ge(S.lc1, 16)
    mm(blk(T.pc, 1), tab(1, pseq[1]), False, True, S.tpc)
    mm(blk(T.pc, 0), tab(1, pseq[0]), True, True, S.tpc)
    te.wait_ge(S.lh0, 16)
    mm(blk(T.ph, 0, 2), tab(0, hb[0], 2), True, False)
    te.wait_ge(S.lh1, 16)
    mm(blk(T.ph, 0, 2), tab(1, hb[0], 2), False, True, S.tph)
    te.wait_ge(S.lm0, 16)
    mm(blk(T.pm0, 0), tab(0, seq[0]), True, False)
    mm(blk(T.pm1, 0), tab(0, seq[1]), True, False)
    te.wait_ge(S.xraw, n_on)
    mm(blk(T.pm0, 0), T.rawl[:, :], False, False)
    te.wait_ge(S.lm1, 16)
    mm(blk(T.pm0, 0), tab(1, seq[0]), False, False)
    mm(blk(T.pm1, 0), tab(1, seq[1]), False, False)
    te.wait_ge(S.lm2, 16)
    mm(blk(T.pm0, 0), tab(2, seq[0]), False, True, S.tpm0)
    mm(blk(T.pm1, 0), tab(2, seq[1]), False, True, S.tpm1)
    te.wait_ge(S.lo0, 16)
    mm(blk(T.pp, 0), tab(0, peer), True, False)
    mm(blk(T.po, 0), tab(0, rank), True, False)
    te.wait_ge(S.lo1, 16)
    mm(blk(T.pp, 0), tab(1, peer), False, True, S.tpp)
    mm(blk(T.po, 0), tab(1, rank), False, False)
    te.wait_ge(S.lo2, 16)
    mm(blk(T.po, 0), tab(2, rank), False, True, S.tpo)

    g.wait_ge(S.lraw, 16)
    send(pcore, T.rawl[:, :], T.raws[:, :], S.xraw, on_mask)

    v.wait_ge(S.tpc, 2)
    v.wait_ge(S.lc2, 16)
    for p in range(2):
        vadd(blk(T.st, p), blk(T.pc, p), tab(2, pseq[p]), S.sst)
    g.wait_ge(S.sst, 2)
    send(pcore, T.xl[:, :], T.st[:, :], S.x1, on_mask)

    v.wait_ge(S.tph, 1)
    v.wait_ge(S.lh2, 16)
    for p in range(2):
        vadd(blk(T.sth, p), blk(T.ph, p), tab(2, hb[p]), S["ssh%d" % p])
        g.wait_ge(S["ssh%d" % p], 1)
        send(hcore, blk(T.hl, 2 * pos_me + p), blk(T.sth, p), S["h%d%d" % (pos_me, p)], h_mask)

    v.wait_ge(S.x1, n_on)
    for p in range(2):
        v.wait_ge(S["tpm%d" % p], 1)
        vadd(blk(T.out, p), blk(T["pm%d" % p], 0), blk(T.xl, p), S["os%d" % p])
        g.wait_ge(S["os%d" % p], 1)
        s = slot[(rank, seq[p])]
        send(cores[seq[p]], blk(T.al, s), blk(T.out, p), S["ar%d" % s], off_mask)

    v.wait_ge(S.tpp, 1)
    v.wait_ge(S.lo2, 16)
    vadd(T.st2[:, :], blk(T.pp, 0), tab(2, peer), S.sst2)
    g.wait_ge(S.sst2, 1)
    send(pcore, T.xl2[:, :], T.st2[:, :], S.x2, on_mask)

    v.wait_ge(S.tpo, 1)
    v.wait_ge(S.x2, n_on)
    vadd(blk(T.pa, 0), blk(T.po, 0), T.xl2[:, :])
    for s in range(3):
        v.wait_ge(S["ar%d" % s], need[(rank, s)])
        v.wait_ge(S.vq, nv[0])
        if s < 2:
            vadd(blk(T.pa, s + 1), blk(T.pa, s), blk(T.al, s))
        else:
            vadd(T.acc[:, :], blk(T.pa, s), blk(T.al, s), S.sacc)

    g.sync.wait_ge(S.sacc, 1)
    g.sync.dma_start(out=T.y[:, :], in_=T.acc[:, :]).then_inc(S.stored, 16)
    g.wait_ge(S.sent, sent[0])
    g.wait_ge(S.stored, 16)
